import numpy as np
import ml_dtypes


def mxq(x, axis, fmt="e4m3"):
    dtype, down = {"e4m3": (ml_dtypes.float8_e4m3fn, 7), "e5m2": (ml_dtypes.float8_e5m2, 14)}[fmt]
    v = np.moveaxis(np.asarray(x, np.float32).astype(ml_dtypes.bfloat16).astype(np.float64), axis, -1)
    blocks = v.reshape(v.shape[:-1] + (-1, 32))
    amax = np.abs(blocks).max(-1, keepdims=True)
    byte = np.maximum(np.where(amax > 0, np.frexp(amax)[1] - 1 + 127, 0) - down, 1)
    scale = np.exp2(byte - 127.0)
    codes = (blocks / scale).astype(np.float32).astype(dtype).astype(np.float64)
    return np.moveaxis((codes * scale).reshape(v.shape), -1, axis)


WIDE = False


def mx_kscale(k):
    if not WIDE:
        return np.ones(k)
    levels = np.array([10, -10, 5, -5, 0])
    if k % 512:
        return np.exp2(np.random.permutation(np.resize(levels, k // 32))).repeat(32)
    a = np.empty((k // 512, 16))
    for p in range(k // 512):
        a[p, :8] = np.random.permutation(np.resize(levels, 8))
        for g in range(8):
            far = levels[np.abs(levels - a[p, g]) >= 10]
            a[p, g + 8] = far[np.random.randint(len(far))]
    return np.exp2(a.ravel()).repeat(32)


def f64(x):
    return np.asarray(x).astype(np.float64)


def striped(idx):
    return np.tile(np.asarray(idx).reshape(-1, 16).T, (8, 1)).astype(np.uint16)


def unstriped(offs):
    return offs[:16].T.reshape(-1).astype(np.int64)


E2M1 = np.array([0.0, 0.5, 1.0, 1.5, 2.0, 3.0, 4.0, 6.0, -0.0, -0.5, -1.0, -1.5, -2.0, -3.0, -4.0, -6.0])


def pack_weight(w, fmt):
    k, n = w.shape
    w = f64(np.asarray(w, np.float32).astype(ml_dtypes.bfloat16)).reshape(k // 32, 32, n)
    amax = np.abs(w).max(1)
    if fmt == "e4m3":
        byte = np.frexp(amax)[1] - 1 + 127 - 7
    else:
        mant, ex = np.frexp(amax / 6.0)
        byte = np.where(mant > 0.5, ex, ex - 1) + 127
    byte = np.clip(np.where(amax > 0, byte, 1), 1, 254)
    scaled = (w * np.exp2(127.0 - byte)[:, None, :]).reshape(k, n).astype(np.float32)
    by_word = np.ascontiguousarray(scaled.reshape(k // 512, 128, 4, n).transpose(0, 1, 3, 2))
    if fmt == "e4m3":
        words = by_word.astype(ml_dtypes.float8_e4m3fn).view(np.uint8)
    else:
        c = by_word.astype(ml_dtypes.float4_e2m1fn).view(np.uint8) & 0xF
        words = (c[..., 0::2] | (c[..., 1::2] << 4)).reshape(k // 512, 128, 2 * n)
    return np.ascontiguousarray(words), np.ascontiguousarray(byte.astype(np.uint8).reshape(k // 512, 16, n))


def unpack_weight(words, scales, fmt):
    g, _, n = scales.shape
    words = np.ascontiguousarray(words).reshape(g, 128, n, -1)
    if fmt == "e4m3":
        vals = words.view(ml_dtypes.float8_e4m3fn).astype(np.float64)
    else:
        nib = np.empty((g, 128, n, 4), np.uint8)
        nib[..., 0::2] = words & 0xF
        nib[..., 1::2] = words >> 4
        vals = E2M1[nib]
    vals = vals * np.repeat(np.exp2(scales.astype(np.float64) - 127.0), 8, axis=1)[..., None]
    return vals.transpose(0, 1, 3, 2).reshape(g * 512, n)


def bf(x):
    return np.asarray(x, np.float32).astype(ml_dtypes.bfloat16)


def planes(Y):
    r, m = Y.shape
    b = f64(bf(Y)).reshape(r // 32, 32, m)
    amax = np.abs(b).max(1)
    byte = np.clip(np.where(amax > 0, np.frexp(amax)[1] - 1 + 127 - 7, 1), 1, 254)
    codes = (b * np.exp2(127.0 - byte)[:, None, :]).reshape(r, m).astype(np.float32).astype(ml_dtypes.float8_e4m3fn).view(np.uint8)
    words = codes.reshape(r // 512, 128, 4, m).transpose(0, 1, 3, 2)
    return np.ascontiguousarray(words), np.ascontiguousarray(byte.astype(np.uint8).reshape(r // 512, 16, m))


K, L, T, J, N = 1024, 512, 2048, 512, 512


def setup_inputs():
    n = np.random.standard_normal
    idx = np.random.permutation(T)[:J]
    fk = mx_kscale(K)
    fl = mx_kscale(L)
    wap = pack_weight(n((K, N)) * 1 / np.sqrt(K) * fk[:, None], "e2m1")
    xbp = pack_weight(n((L, J)) / fl[:, None], "e4m3")
    wbp = pack_weight(n((L, N)) * 1 / np.sqrt(L) * fl[:, None], "e2m1")
    return {
        "xa": (n((K, T)) / fk[:, None]).astype(np.float32),
        "wa_words": wap[0],
        "wa_scales": wap[1],
        "xb_words": xbp[0],
        "xb_scales": xbp[1],
        "wb_words": wbp[0],
        "wb_scales": wbp[1],
        "offs": striped(idx),
    }


def reference(xa, wa_words, wa_scales, xb_words, xb_scales, wb_words, wb_scales, offs):
    idx = unstriped(offs)
    wau = unpack_weight(wa_words, wa_scales, "e2m1")
    xbu = unpack_weight(xb_words, xb_scales, "e4m3")
    wbu = unpack_weight(wb_words, wb_scales, "e2m1")
    xaidxq = mxq(f64(xa)[:, idx], 0, "e4m3")
    p = wau.T @ xaidxq
    q = wbu.T @ xbu
    y = np.maximum(p, q) - 0.25 * (p + q)
    words, scales = planes(y)
    return y, words, scales

@@ -1,0 +1,197 @@
+from contextlib import ExitStack
+
+import concourse.mybir as mybir
+
+K, L, T, J, N = 1024, 512, 2048, 512, 512
+FLOPS = 2 * (K + L) * N * J
+
+F32 = mybir.dt.float32
+BF16 = mybir.dt.bfloat16
+I32 = mybir.dt.int32
+U32 = mybir.dt.uint32
+U16 = mybir.dt.uint16
+U8 = mybir.dt.uint8
+FP8X4 = mybir.dt.float8_e4m3fn_x4
+FP4X4 = mybir.dt.float4_e2m1fn_x4
+ALU = mybir.AluOpType
+ACT = mybir.ActivationFunctionType
+
+P = 128
+PACK = 4
+K_PASS = P * PACK
+PASSES = K // K_PASS
+QUADS = 4
+SLICE = 128
+SLICES = J // SLICE
+HALF = J // 2
+WB = PASSES
+XB = PASSES + 1
+
+
+def tile_list_better_of_two_views_pl_kernel(
+    tc, xa, wa_words, wa_scales, xb_words, xb_scales, wb_words, wb_scales, offs, out_0, out_1, out_2
+):
+    nc = tc.nc
+    with ExitStack() as ctx:
+        keep = ctx.enter_context(tc.tile_pool(name="keep", bufs=1))
+        ring = ctx.enter_context(tc.tile_pool(name="ring", bufs=4))
+        psum = ctx.enter_context(tc.psum_pool(name="psum", bufs=1))
+
+        offsets = keep.tile([P, J // 16], U16, name="offsets")
+        w_raw = keep.tile([P, PASSES + 1, 2 * N], U8, name="w_raw", align_bytes=64)
+        w_dealt = keep.tile([P, PASSES + 1, 2 * N], U8, name="w_dealt", align_bytes=64)
+        s_stage = keep.tile([16, PASSES + 2, N], U8, name="s_stage", align_bytes=64)
+        s_raw = keep.tile([P, PASSES + 2, N], U8, name="s_raw", align_bytes=64)
+        xb_codes = keep.tile([P, J], U32, name="xb_codes", align_bytes=64)
+
+        nc.gpsimd.memset(s_raw[:].rearrange("p a n -> p (a n)").bitcast(U32), 0)
+
+        nc.sync.dma_start(
+            w_raw[:, 0:PASSES, :].bitcast(I32), wa_words.rearrange("a p n -> p a n").bitcast(I32)
+        )
+        nc.sync.dma_start(w_raw[:, WB, :].bitcast(I32), wb_words[0].bitcast(I32))
+        nc.scalar.dma_start(
+            s_stage[:, 0:PASSES, :].bitcast(I32), wa_scales.rearrange("a q n -> q a n").bitcast(I32)
+        )
+        nc.scalar.dma_start(s_stage[:, WB, :].bitcast(I32), wb_scales[0].bitcast(I32))
+        nc.scalar.dma_start(s_stage[:, XB, :].bitcast(I32), xb_scales[0].bitcast(I32))
+        nc.sync.dma_start(offsets[:], offs)
+
+        rows = xa.rearrange("(a p t) c -> a t p c", a=PASSES, t=PACK)
+        picked = [keep.tile([P, J, PACK], BF16, name="picked%d" % a, align_bytes=64) for a in range(PASSES)]
+        xa_codes = [keep.tile([P, J], U32, name="xa_codes%d" % a, align_bytes=64) for a in range(PASSES)]
+        xa_scales = [keep.tile([P, J], U8, name="xa_scales%d" % a, align_bytes=64) for a in range(PASSES)]
+
+        def load(a, t):
+            window = ring.tile([P, T], F32, name="window")
+            nc.sync.dma_start(window[:], rows[a, t])
+            return window
+
+        def gather(window, pair, t, cols):
+            nc.vector.tensor_copy(
+                pair[:, t % 2, cols], window[:].indirect(offsets[:, cols.start // 16 : cols.stop // 16])
+            )
+
+        def weave(a, u, pair, cols):
+            nc.scalar.copy(picked[a][:, cols, 2 * u : 2 * u + 2], pair[:, :, cols].rearrange("p e j -> p j e"))
+
+        def quantise(a, cols):
+            nc.vector.quantize_mx(
+                out=xa_codes[a][:, cols].bitcast(FP8X4),
+                scales=xa_scales[a][:, cols],
+                in_=picked[a][:, cols, :].rearrange("p j t -> p (j t)"),
+            )
+
+        def new_pair(a, u):
+            return keep.tile([P, 2, J], BF16, name="pair%d%d" % (a, u), tag="pair%d%d" % (a, u), align_bytes=64)
+
+        whole = slice(0, J)
+        first_windows = [load(0, 0), load(0, 1)]
+        nc.sync.dma_start(xb_codes[:].bitcast(I32), xb_words[0].rearrange("p n t -> p (n t)").bitcast(I32))
+        for quad in range(QUADS):
+            nc.scalar.dma_start(
+                s_raw[32 * quad : 32 * quad + 4].rearrange("p a n -> p (a n)").bitcast(I32),
+                s_stage[4 * quad : 4 * quad + 4].rearrange("p a n -> p (a n)").bitcast(I32),
+            )
+        nc.vector.tensor_copy(
+            w_dealt[:].bitcast(U16).rearrange("p a (t m) -> p a t m", t=PACK),
+            w_raw[:].bitcast(U16).rearrange("p a (m t) -> p a t m", t=PACK),
+        )
+
+        pair = new_pair(0, 0)
+        for t in range(2):
+            gather(first_windows[t], pair, t, whole)
+        weave(0, 0, pair, whole)
+
+        s_dealt = keep.tile([P, PASSES + 1, N], U8, name="s_dealt", tag="pair00", align_bytes=64)
+        nc.vector.tensor_copy(
+            s_dealt[:].rearrange("p a (t m) -> p a t m", t=PACK),
+            s_raw[:, 0 : PASSES + 1, :].rearrange("p a (m t) -> p a t m", t=PACK),
+        )
+
+        def product(out, plane, t, codes, scales, start, stop):
+            nc.tensor.matmul_mx(
+                out=out,
+                lhsT=w_dealt[:, plane, 2 * P * t : 2 * P * (t + 1)].bitcast(FP4X4),
+                lhsT_scale=s_dealt[:, plane, P * t : P * (t + 1)],
+                rhs=codes.bitcast(FP8X4),
+                rhs_scale=scales,
+                start=start,
+                stop=stop,
+            )
+
+        q_sb = keep.tile([P, SLICES, PACK, SLICE], F32, name="q_sb")
+        for t in range(PACK):
+            q_bank = psum.tile([P, J], F32, name="q_bank%d" % t)
+            product(q_bank[:], WB, t, xb_codes[:], s_raw[:, XB, :], True, True)
+            nc.scalar.copy(q_sb[:, :, t, :], q_bank[:].rearrange("p (c j) -> p c j", j=SLICE))
+
+        banks = [psum.tile([P, PACK, SLICE], F32, name="bank%d" % c) for c in range(SLICES)]
+        for c in range(1, SLICES):
+            cols = slice(SLICE * c, SLICE * (c + 1))
+            for t in range(PACK):
+                product(banks[c][:, t, :], WB, t, xb_codes[:, cols], s_raw[:, XB, cols], t == 0, False)
+
+        pair = new_pair(0, 1)
+        for t in range(2, PACK):
+            gather(load(0, t), pair, t, whole)
+        weave(0, 1, pair, whole)
+        quantise(0, whole)
+        for c in range(SLICES):
+            cols = slice(SLICE * c, SLICE * (c + 1))
+            for t in range(PACK):
+                product(banks[c][:, t, :], 0, t, xa_codes[0][:, cols], xa_scales[0][:, cols], c == 0 and t == 0, False)
+
+        pair = new_pair(1, 0)
+        for t in range(2):
+            gather(load(1, t), pair, t, whole)
+        weave(1, 0, pair, whole)
+        pair = new_pair(1, 1)
+        gather(load(1, 2), pair, 2, whole)
+        last_window = load(1, 3)
+        for c in range(SLICES):
+            gather(last_window, pair, 3, slice(SLICE * c, SLICE * (c + 1)))
+        for c in range(SLICES):
+            cols = slice(SLICE * c, SLICE * (c + 1))
+            weave(1, 1, pair, cols)
+            quantise(1, cols)
+            for t in range(PACK):
+                product(banks[c][:, t, :], 1, t, xa_codes[1][:, cols], xa_scales[1][:, cols], False, t == PACK - 1)
+
+        y_codes = keep.tile([P, J], U32, name="y_codes", align_bytes=64)
+        y_scales = keep.tile([P, J], U8, name="y_scales", align_bytes=64)
+        out_rows = out_0.rearrange("(p t) j -> p t j", t=PACK)
+        out_words = out_1[0].rearrange("p n t -> p (n t)").bitcast(I32)
+        for c in range(SLICES):
+            cols = slice(SLICE * c, SLICE * (c + 1))
+            y = keep.tile([P, PACK, SLICE], F32, name="y%d" % c)
+            first = keep.tile([P, PACK, SLICE], F32, name="first%d" % c)
+            second = keep.tile([P, PACK, SLICE], F32, name="second%d" % c)
+            if c == 0:
+                nc.vector.tensor_tensor(first[:], banks[c][:], q_sb[:, c], ALU.max)
+                nc.vector.tensor_tensor(second[:], banks[c][:], q_sb[:, c], ALU.add)
+                nc.vector.scalar_tensor_tensor(y[:], second[:], -0.25, first[:], ALU.mult, ALU.add)
+            else:
+                nc.vector.scalar_tensor_tensor(first[:], banks[c][:], 0.5, q_sb[:, c], ALU.mult, ALU.subtract)
+                nc.scalar.activation(second[:], first[:], ACT.Abs)
+                nc.vector.scalar_tensor_tensor(y[:], banks[c][:], 0.25, second[:], ALU.mult, ALU.add)
+            nc.sync.dma_start(out_rows[:, :, cols], y[:])
+            rounded = keep.tile([P, SLICE, PACK], BF16, name="rounded%d" % c, align_bytes=64)
+            nc.scalar.copy(
+                rounded[:].rearrange("p (g i) t -> p g t i", i=4),
+                y[:].rearrange("p t (g i) -> p g t i", i=4),
+            )
+            nc.vector.quantize_mx(
+                out=y_codes[:, cols].bitcast(FP8X4),
+                scales=y_scales[:, cols],
+                in_=rounded[:].rearrange("p j t -> p (j t)"),
+            )
+            if c % 2 == 1:
+                pair = slice(SLICE * (c - 1), SLICE * (c + 1))
+                nc.sync.dma_start(out_words[:, pair], y_codes[:, pair].bitcast(I32))
+        for quad in range(QUADS):
+            queue = nc.sync if quad % 2 == 0 else nc.scalar
+            queue.dma_start(
+                out_2[0, 4 * quad : 4 * quad + 4, :].bitcast(I32),
+                y_scales[32 * quad : 32 * quad + 4, :].bitcast(I32),
+            )

@@ -23,7 +23,6 @@ PASSES = K // K_PASS
 QUADS = 4
 SLICE = 128
 SLICES = J // SLICE
-HALF = J // 2
 WB = PASSES
 XB = PASSES + 1
 
@@ -34,7 +33,7 @@ def tile_list_better_of_two_views_pl_kernel(
     nc = tc.nc
     with ExitStack() as ctx:
         keep = ctx.enter_context(tc.tile_pool(name="keep", bufs=1))
-        ring = ctx.enter_context(tc.tile_pool(name="ring", bufs=4))
+        ring = ctx.enter_context(tc.tile_pool(name="ring", bufs=3))
         psum = ctx.enter_context(tc.psum_pool(name="psum", bufs=1))
 
         offsets = keep.tile([P, J // 16], U16, name="offsets")
@@ -58,35 +57,30 @@ def tile_list_better_of_two_views_pl_kernel(
         nc.sync.dma_start(offsets[:], offs)
 
         rows = xa.rearrange("(a p t) c -> a t p c", a=PASSES, t=PACK)
-        picked = [keep.tile([P, J, PACK], BF16, name="picked%d" % a, align_bytes=64) for a in range(PASSES)]
-        xa_codes = [keep.tile([P, J], U32, name="xa_codes%d" % a, align_bytes=64) for a in range(PASSES)]
-        xa_scales = [keep.tile([P, J], U8, name="xa_scales%d" % a, align_bytes=64) for a in range(PASSES)]
 
-        def load(a, t):
-            window = ring.tile([P, T], F32, name="window")
+        def load(a, t, pool, tag):
+            window = pool.tile([P, T], F32, name="window%d%d" % (a, t), tag=tag, align_bytes=64)
             nc.sync.dma_start(window[:], rows[a, t])
             return window
 
-        def gather(window, pair, t, cols):
-            nc.vector.tensor_copy(
-                pair[:, t % 2, cols], window[:].indirect(offsets[:, cols.start // 16 : cols.stop // 16])
-            )
+        def gather(out, window, cols):
+            nc.vector.tensor_copy(out, window[:].indirect(offsets[:, cols.start // 16 : cols.stop // 16]))
 
-        def weave(a, u, pair, cols):
-            nc.scalar.copy(picked[a][:, cols, 2 * u : 2 * u + 2], pair[:, :, cols].rearrange("p e j -> p j e"))
+        def weave(picked, u, pair):
+            nc.scalar.copy(picked[:, :, 2 * u : 2 * u + 2], pair.rearrange("p e j -> p j e"))
 
-        def quantise(a, cols):
+        def quantise(picked, name, tag):
+            width = picked.shape[1]
+            codes = keep.tile([P, width], U32, name=name + "_codes", tag=tag, align_bytes=64)
+            scales = keep.tile([P, width], U8, name=name + "_scales", align_bytes=64)
             nc.vector.quantize_mx(
-                out=xa_codes[a][:, cols].bitcast(FP8X4),
-                scales=xa_scales[a][:, cols],
-                in_=picked[a][:, cols, :].rearrange("p j t -> p (j t)"),
+                out=codes[:].bitcast(FP8X4), scales=scales[:], in_=picked.rearrange("p j t -> p (j t)")
             )
-
-        def new_pair(a, u):
-            return keep.tile([P, 2, J], BF16, name="pair%d%d" % (a, u), tag="pair%d%d" % (a, u), align_bytes=64)
+            return codes, scales
 
         whole = slice(0, J)
-        first_windows = [load(0, 0), load(0, 1)]
+        slices = [slice(SLICE * c, SLICE * (c + 1)) for c in range(SLICES)]
+        early = [load(0, 0, keep, "twice"), load(0, 1, keep, "once")]
         nc.sync.dma_start(xb_codes[:].bitcast(I32), xb_words[0].rearrange("p n t -> p (n t)").bitcast(I32))
         for quad in range(QUADS):
             nc.scalar.dma_start(
@@ -98,12 +92,11 @@ def tile_list_better_of_two_views_pl_kernel(
             w_raw[:].bitcast(U16).rearrange("p a (m t) -> p a t m", t=PACK),
         )
 
-        pair = new_pair(0, 0)
+        planes = keep.tile([P, PACK, J], BF16, name="planes")
         for t in range(2):
-            gather(first_windows[t], pair, t, whole)
-        weave(0, 0, pair, whole)
+            gather(planes[:, t, :], early[t], whole)
 
-        s_dealt = keep.tile([P, PASSES + 1, N], U8, name="s_dealt", tag="pair00", align_bytes=64)
+        s_dealt = keep.tile([P, PASSES + 1, N], U8, name="s_dealt", tag="once", align_bytes=64)
         nc.vector.tensor_copy(
             s_dealt[:].rearrange("p a (t m) -> p a t m", t=PACK),
             s_raw[:, 0 : PASSES + 1, :].rearrange("p a (m t) -> p a t m", t=PACK),
@@ -125,72 +118,103 @@ def tile_list_better_of_two_views_pl_kernel(
             q_bank = psum.tile([P, J], F32, name="q_bank%d" % t)
             product(q_bank[:], WB, t, xb_codes[:], s_raw[:, XB, :], True, True)
             nc.scalar.copy(q_sb[:, :, t, :], q_bank[:].rearrange("p (c j) -> p c j", j=SLICE))
+        q_quarter = keep.tile([P, PACK, SLICE], F32, name="q_quarter")
+        nc.scalar.activation(q_quarter[:], q_sb[:, 0], ACT.Copy, scale=-0.25)
+        warm = keep.tile([P, 1], F32, name="warm")
+        nc.scalar.activation(warm[:], q_sb[:, 0, 0, 0:1], ACT.Abs)
 
         banks = [psum.tile([P, PACK, SLICE], F32, name="bank%d" % c) for c in range(SLICES)]
         for c in range(1, SLICES):
-            cols = slice(SLICE * c, SLICE * (c + 1))
             for t in range(PACK):
-                product(banks[c][:, t, :], WB, t, xb_codes[:, cols], s_raw[:, XB, cols], t == 0, False)
+                product(banks[c][:, t, :], WB, t, xb_codes[:, slices[c]], s_raw[:, XB, slices[c]], t == 0, False)
 
-        pair = new_pair(0, 1)
         for t in range(2, PACK):
-            gather(load(0, t), pair, t, whole)
-        weave(0, 1, pair, whole)
-        quantise(0, whole)
-        for c in range(SLICES):
-            cols = slice(SLICE * c, SLICE * (c + 1))
-            for t in range(PACK):
-                product(banks[c][:, t, :], 0, t, xa_codes[0][:, cols], xa_scales[0][:, cols], c == 0 and t == 0, False)
+            gather(planes[:, t, :], load(0, t, ring, "ring"), whole)
+        picked = keep.tile([P, J, PACK], BF16, name="picked", align_bytes=64)
+        nc.scalar.copy(
+            picked[:].rearrange("p (g i) t -> p g t i", i=4), planes[:].rearrange("p t (g i) -> p g t i", i=4)
+        )
 
-        pair = new_pair(1, 0)
-        for t in range(2):
-            gather(load(1, t), pair, t, whole)
-        weave(1, 0, pair, whole)
-        pair = new_pair(1, 1)
-        gather(load(1, 2), pair, 2, whole)
-        last_window = load(1, 3)
+        low_pair = keep.tile([P, 2, J], BF16, name="low_pair")
+        gather(low_pair[:, 0, :], load(1, 0, ring, "ring"), whole)
+        gather(low_pair[:, 1, :], load(1, 1, keep, "twice"), whole)
+        codes, scales = quantise(picked[:], "early", "twice")
         for c in range(SLICES):
-            gather(last_window, pair, 3, slice(SLICE * c, SLICE * (c + 1)))
-        for c in range(SLICES):
-            cols = slice(SLICE * c, SLICE * (c + 1))
-            weave(1, 1, pair, cols)
-            quantise(1, cols)
             for t in range(PACK):
-                product(banks[c][:, t, :], 1, t, xa_codes[1][:, cols], xa_scales[1][:, cols], False, t == PACK - 1)
+                product(banks[c][:, t, :], 0, t, codes[:, slices[c]], scales[:, slices[c]], c == 0 and t == 0, False)
 
-        y_codes = keep.tile([P, J], U32, name="y_codes", align_bytes=64)
-        y_scales = keep.tile([P, J], U8, name="y_scales", align_bytes=64)
+        late = [
+            keep.tile([P, SLICE, PACK], BF16, name="late%d" % c, tag="late%d" % c, align_bytes=64)
+            for c in range(SLICES)
+        ]
+        for c in range(SLICES):
+            weave(late[c][:], 0, low_pair[:, :, slices[c]])
+        high_pairs = [keep.tile([P, 2, SLICE], BF16, name="high_pair%d" % c) for c in range(SLICES)]
+        for t in range(2, PACK):
+            window = load(1, t, ring, "ring")
+            for c in range(SLICES):
+                gather(high_pairs[c][:, t - 2, :], window, slices[c])
+        for c in range(SLICES):
+            weave(late[c][:], 1, high_pairs[c][:])
+            codes, scales = quantise(late[c][:], "late%d" % c, "late_codes%d" % c)
+            for t in range(PACK):
+                product(banks[c][:, t, :], 1, t, codes[:], scales[:], False, t == PACK - 1)
+
         out_rows = out_0.rearrange("(p t) j -> p t j", t=PACK)
         out_words = out_1[0].rearrange("p n t -> p (n t)").bitcast(I32)
-        for c in range(SLICES):
-            cols = slice(SLICE * c, SLICE * (c + 1))
-            y = keep.tile([P, PACK, SLICE], F32, name="y%d" % c)
-            first = keep.tile([P, PACK, SLICE], F32, name="first%d" % c)
-            second = keep.tile([P, PACK, SLICE], F32, name="second%d" % c)
-            if c == 0:
-                nc.vector.tensor_tensor(first[:], banks[c][:], q_sb[:, c], ALU.max)
-                nc.vector.tensor_tensor(second[:], banks[c][:], q_sb[:, c], ALU.add)
-                nc.vector.scalar_tensor_tensor(y[:], second[:], -0.25, first[:], ALU.mult, ALU.add)
-            else:
-                nc.vector.scalar_tensor_tensor(first[:], banks[c][:], 0.5, q_sb[:, c], ALU.mult, ALU.subtract)
-                nc.scalar.activation(second[:], first[:], ACT.Abs)
-                nc.vector.scalar_tensor_tensor(y[:], banks[c][:], 0.25, second[:], ALU.mult, ALU.add)
-            nc.sync.dma_start(out_rows[:, :, cols], y[:])
-            rounded = keep.tile([P, SLICE, PACK], BF16, name="rounded%d" % c, align_bytes=64)
+        y = [keep.tile([P, PACK, SLICE], F32, name="y%d" % c) for c in range(SLICES)]
+        first = [keep.tile([P, PACK, SLICE], F32, name="first%d" % c) for c in range(SLICES)]
+        second = [keep.tile([P, PACK, SLICE], F32, name="second%d" % c) for c in range(SLICES)]
+        rounded = keep.tile([P, J, PACK], BF16, name="rounded", align_bytes=64)
+        y_codes = keep.tile([P, J], U32, name="y_codes", align_bytes=64)
+        y_scales = keep.tile([P, J], U8, name="y_scales", align_bytes=64)
+
+        def gap(c):
+            nc.vector.scalar_tensor_tensor(first[c][:], banks[c][:], 0.5, q_sb[:, c], ALU.mult, ALU.subtract)
+            nc.scalar.activation(second[c][:], first[c][:], ACT.Abs)
+
+        def combine(c):
+            nc.vector.scalar_tensor_tensor(y[c][:], banks[c][:], 0.25, second[c][:], ALU.mult, ALU.add)
+            nc.sync.dma_start(out_rows[:, :, slices[c]], y[c][:])
+
+        def round_once(c):
             nc.scalar.copy(
-                rounded[:].rearrange("p (g i) t -> p g t i", i=4),
-                y[:].rearrange("p t (g i) -> p g t i", i=4),
+                rounded[:, slices[c], :].rearrange("p (g i) t -> p g t i", i=4),
+                y[c][:].rearrange("p t (g i) -> p g t i", i=4),
             )
+
+        def quantise_y(cols):
             nc.vector.quantize_mx(
                 out=y_codes[:, cols].bitcast(FP8X4),
                 scales=y_scales[:, cols],
-                in_=rounded[:].rearrange("p j t -> p (j t)"),
+                in_=rounded[:, cols, :].rearrange("p j t -> p (j t)"),
             )
-            if c % 2 == 1:
-                pair = slice(SLICE * (c - 1), SLICE * (c + 1))
-                nc.sync.dma_start(out_words[:, pair], y_codes[:, pair].bitcast(I32))
+
+        nc.vector.tensor_tensor(first[0][:], banks[0][:], q_sb[:, 0], ALU.max)
+        nc.vector.scalar_tensor_tensor(second[0][:], banks[0][:], -0.25, q_quarter[:], ALU.mult, ALU.add)
+        nc.gpsimd.tensor_tensor(y[0][:], first[0][:], second[0][:], ALU.add)
+        nc.sync.dma_start(out_rows[:, :, slices[0]], y[0][:])
+        nc.gpsimd.tensor_scalar(
+            rounded[:, slices[0], :], y[0][:].rearrange("p t j -> p j t"), 1.0, 0.0, ALU.mult, ALU.add
+        )
+        gap(1)
+        gap(2)
+        combine(1)
+        gap(3)
+        round_once(1)
+        combine(2)
+        combine(3)
+        round_once(2)
+        round_once(3)
+        half = slice(0, J // 2)
+        quantise_y(half)
+        nc.sync.dma_start(out_words[:, half], y_codes[:, half].bitcast(I32))
+        for c in range(2, SLICES):
+            quantise_y(slices[c])
+        half = slice(J // 2, J)
+        nc.sync.dma_start(out_words[:, half], y_codes[:, half].bitcast(I32))
         for quad in range(QUADS):
-            queue = nc.sync if quad % 2 == 0 else nc.scalar
+            queue = nc.sync if quad % 2 == 1 else nc.scalar
             queue.dma_start(
                 out_2[0, 4 * quad : 4 * quad + 4, :].bitcast(I32),
                 y_scales[32 * quad : 32 * quad + 4, :].bitcast(I32),

from contextlib import ExitStack

import concourse.mybir as mybir

K, L, T, J, N = 1024, 512, 2048, 512, 512
FLOPS = 2 * (K + L) * N * J

F32 = mybir.dt.float32
BF16 = mybir.dt.bfloat16
I32 = mybir.dt.int32
U32 = mybir.dt.uint32
U16 = mybir.dt.uint16
U8 = mybir.dt.uint8
FP8X4 = mybir.dt.float8_e4m3fn_x4
FP4X4 = mybir.dt.float4_e2m1fn_x4
ALU = mybir.AluOpType
ACT = mybir.ActivationFunctionType

P = 128
PACK = 4
K_PASS = P * PACK
PASSES = K // K_PASS
QUADS = 4
SLICE = 128
SLICES = J // SLICE
WB = PASSES
XB = PASSES + 1


def tile_list_better_of_two_views_pl_kernel(
    tc, xa, wa_words, wa_scales, xb_words, xb_scales, wb_words, wb_scales, offs, out_0, out_1, out_2
):
    nc = tc.nc
    with ExitStack() as ctx:
        keep = ctx.enter_context(tc.tile_pool(name="keep", bufs=1))
        ring = ctx.enter_context(tc.tile_pool(name="ring", bufs=3))
        psum = ctx.enter_context(tc.psum_pool(name="psum", bufs=1))

        offsets = keep.tile([P, J // 16], U16, name="offsets")
        w_raw = keep.tile([P, PASSES + 1, 2 * N], U8, name="w_raw", align_bytes=64)
        w_dealt = keep.tile([P, PASSES + 1, 2 * N], U8, name="w_dealt", align_bytes=64)
        s_stage = keep.tile([16, PASSES + 2, N], U8, name="s_stage", align_bytes=64)
        s_raw = keep.tile([P, PASSES + 2, N], U8, name="s_raw", align_bytes=64)
        xb_codes = keep.tile([P, J], U32, name="xb_codes", align_bytes=64)

        nc.gpsimd.memset(s_raw[:].rearrange("p a n -> p (a n)").bitcast(U32), 0)

        nc.sync.dma_start(
            w_raw[:, 0:PASSES, :].bitcast(I32), wa_words.rearrange("a p n -> p a n").bitcast(I32)
        )
        nc.sync.dma_start(w_raw[:, WB, :].bitcast(I32), wb_words[0].bitcast(I32))
        nc.scalar.dma_start(
            s_stage[:, 0:PASSES, :].bitcast(I32), wa_scales.rearrange("a q n -> q a n").bitcast(I32)
        )
        nc.scalar.dma_start(s_stage[:, WB, :].bitcast(I32), wb_scales[0].bitcast(I32))
        nc.scalar.dma_start(s_stage[:, XB, :].bitcast(I32), xb_scales[0].bitcast(I32))
        nc.sync.dma_start(offsets[:], offs)

        rows = xa.rearrange("(a p t) c -> a t p c", a=PASSES, t=PACK)

        def load(a, t, pool, tag):
            window = pool.tile([P, T], F32, name="window%d%d" % (a, t), tag=tag, align_bytes=64)
            nc.sync.dma_start(window[:], rows[a, t])
            return window

        def gather(out, window, cols):
            nc.vector.tensor_copy(out, window[:].indirect(offsets[:, cols.start // 16 : cols.stop // 16]))

        def weave(picked, u, pair):
            nc.scalar.copy(picked[:, :, 2 * u : 2 * u + 2], pair.rearrange("p e j -> p j e"))

        def quantise(picked, name, tag):
            width = picked.shape[1]
            codes = keep.tile([P, width], U32, name=name + "_codes", tag=tag, align_bytes=64)
            scales = keep.tile([P, width], U8, name=name + "_scales", align_bytes=64)
            nc.vector.quantize_mx(
                out=codes[:].bitcast(FP8X4), scales=scales[:], in_=picked.rearrange("p j t -> p (j t)")
            )
            return codes, scales

        whole = slice(0, J)
        slices = [slice(SLICE * c, SLICE * (c + 1)) for c in range(SLICES)]
        early = [load(0, 0, keep, "twice"), load(0, 1, keep, "once")]
        nc.sync.dma_start(xb_codes[:].bitcast(I32), xb_words[0].rearrange("p n t -> p (n t)").bitcast(I32))
        for quad in range(QUADS):
            nc.scalar.dma_start(
                s_raw[32 * quad : 32 * quad + 4].rearrange("p a n -> p (a n)").bitcast(I32),
                s_stage[4 * quad : 4 * quad + 4].rearrange("p a n -> p (a n)").bitcast(I32),
            )
        nc.vector.tensor_copy(
            w_dealt[:].bitcast(U16).rearrange("p a (t m) -> p a t m", t=PACK),
            w_raw[:].bitcast(U16).rearrange("p a (m t) -> p a t m", t=PACK),
        )

        planes = keep.tile([P, PACK, J], BF16, name="planes")
        for t in range(2):
            gather(planes[:, t, :], early[t], whole)

        s_dealt = keep.tile([P, PASSES + 1, N], U8, name="s_dealt", tag="once", align_bytes=64)
        nc.vector.tensor_copy(
            s_dealt[:].rearrange("p a (t m) -> p a t m", t=PACK),
            s_raw[:, 0 : PASSES + 1, :].rearrange("p a (m t) -> p a t m", t=PACK),
        )

        def product(out, plane, t, codes, scales, start, stop):
            nc.tensor.matmul_mx(
                out=out,
                lhsT=w_dealt[:, plane, 2 * P * t : 2 * P * (t + 1)].bitcast(FP4X4),
                lhsT_scale=s_dealt[:, plane, P * t : P * (t + 1)],
                rhs=codes.bitcast(FP8X4),
                rhs_scale=scales,
                start=start,
                stop=stop,
            )

        q_sb = keep.tile([P, SLICES, PACK, SLICE], F32, name="q_sb")
        for t in range(PACK):
            q_bank = psum.tile([P, J], F32, name="q_bank%d" % t)
            product(q_bank[:], WB, t, xb_codes[:], s_raw[:, XB, :], True, True)
            nc.scalar.copy(q_sb[:, :, t, :], q_bank[:].rearrange("p (c j) -> p c j", j=SLICE))
        q_quarter = keep.tile([P, PACK, SLICE], F32, name="q_quarter")
        nc.scalar.activation(q_quarter[:], q_sb[:, 0], ACT.Copy, scale=-0.25)
        warm = keep.tile([P, 1], F32, name="warm")
        nc.scalar.activation(warm[:], q_sb[:, 0, 0, 0:1], ACT.Abs)

        banks = [psum.tile([P, PACK, SLICE], F32, name="bank%d" % c) for c in range(SLICES)]
        for c in range(1, SLICES):
            for t in range(PACK):
                product(banks[c][:, t, :], WB, t, xb_codes[:, slices[c]], s_raw[:, XB, slices[c]], t == 0, False)

        for t in range(2, PACK):
            gather(planes[:, t, :], load(0, t, ring, "ring"), whole)
        picked = keep.tile([P, J, PACK], BF16, name="picked", align_bytes=64)
        nc.scalar.copy(
            picked[:].rearrange("p (g i) t -> p g t i", i=4), planes[:].rearrange("p t (g i) -> p g t i", i=4)
        )

        low_pair = keep.tile([P, 2, J], BF16, name="low_pair")
        gather(low_pair[:, 0, :], load(1, 0, ring, "ring"), whole)
        gather(low_pair[:, 1, :], load(1, 1, keep, "twice"), whole)
        codes, scales = quantise(picked[:], "early", "twice")
        for c in range(SLICES):
            for t in range(PACK):
                product(banks[c][:, t, :], 0, t, codes[:, slices[c]], scales[:, slices[c]], c == 0 and t == 0, False)

        late = [
            keep.tile([P, SLICE, PACK], BF16, name="late%d" % c, tag="late%d" % c, align_bytes=64)
            for c in range(SLICES)
        ]
        for c in range(SLICES):
            weave(late[c][:], 0, low_pair[:, :, slices[c]])
        high_pairs = [keep.tile([P, 2, SLICE], BF16, name="high_pair%d" % c) for c in range(SLICES)]
        for t in range(2, PACK):
            window = load(1, t, ring, "ring")
            for c in range(SLICES):
                gather(high_pairs[c][:, t - 2, :], window, slices[c])
        for c in range(SLICES):
            weave(late[c][:], 1, high_pairs[c][:])
            codes, scales = quantise(late[c][:], "late%d" % c, "late_codes%d" % c)
            for t in range(PACK):
                product(banks[c][:, t, :], 1, t, codes[:], scales[:], False, t == PACK - 1)

        out_rows = out_0.rearrange("(p t) j -> p t j", t=PACK)
        out_words = out_1[0].rearrange("p n t -> p (n t)").bitcast(I32)
        y = [keep.tile([P, PACK, SLICE], F32, name="y%d" % c) for c in range(SLICES)]
        first = [keep.tile([P, PACK, SLICE], F32, name="first%d" % c) for c in range(SLICES)]
        second = [keep.tile([P, PACK, SLICE], F32, name="second%d" % c) for c in range(SLICES)]
        rounded = keep.tile([P, J, PACK], BF16, name="rounded", align_bytes=64)
        y_codes = keep.tile([P, J], U32, name="y_codes", align_bytes=64)
        y_scales = keep.tile([P, J], U8, name="y_scales", align_bytes=64)

        def gap(c):
            nc.vector.scalar_tensor_tensor(first[c][:], banks[c][:], 0.5, q_sb[:, c], ALU.mult, ALU.subtract)
            nc.scalar.activation(second[c][:], first[c][:], ACT.Abs)

        def combine(c):
            nc.vector.scalar_tensor_tensor(y[c][:], banks[c][:], 0.25, second[c][:], ALU.mult, ALU.add)
            nc.sync.dma_start(out_rows[:, :, slices[c]], y[c][:])

        def round_once(c):
            nc.scalar.copy(
                rounded[:, slices[c], :].rearrange("p (g i) t -> p g t i", i=4),
                y[c][:].rearrange("p t (g i) -> p g t i", i=4),
            )

        def quantise_y(cols):
            nc.vector.quantize_mx(
                out=y_codes[:, cols].bitcast(FP8X4),
                scales=y_scales[:, cols],
                in_=rounded[:, cols, :].rearrange("p j t -> p (j t)"),
            )

        nc.vector.tensor_tensor(first[0][:], banks[0][:], q_sb[:, 0], ALU.max)
        nc.vector.scalar_tensor_tensor(second[0][:], banks[0][:], -0.25, q_quarter[:], ALU.mult, ALU.add)
        nc.gpsimd.tensor_tensor(y[0][:], first[0][:], second[0][:], ALU.add)
        nc.sync.dma_start(out_rows[:, :, slices[0]], y[0][:])
        nc.gpsimd.tensor_scalar(
            rounded[:, slices[0], :], y[0][:].rearrange("p t j -> p j t"), 1.0, 0.0, ALU.mult, ALU.add
        )
        gap(1)
        gap(2)
        combine(1)
        gap(3)
        round_once(1)
        combine(2)
        combine(3)
        round_once(2)
        round_once(3)
        half = slice(0, J // 2)
        quantise_y(half)
        nc.sync.dma_start(out_words[:, half], y_codes[:, half].bitcast(I32))
        for c in range(2, SLICES):
            quantise_y(slices[c])
        half = slice(J // 2, J)
        nc.sync.dma_start(out_words[:, half], y_codes[:, half].bitcast(I32))
        for quad in range(QUADS):
            queue = nc.sync if quad % 2 == 1 else nc.scalar
            queue.dma_start(
                out_2[0, 4 * quad : 4 * quad + 4, :].bitcast(I32),
                y_scales[32 * quad : 32 * quad + 4, :].bitcast(I32),
            )
